import numpy as np
import ml_dtypes


def mxq(x, axis, fmt="e4m3"):
    dtype, down = {"e4m3": (ml_dtypes.float8_e4m3fn, 7), "e5m2": (ml_dtypes.float8_e5m2, 14)}[fmt]
    v = np.moveaxis(np.asarray(x, np.float32).astype(ml_dtypes.bfloat16).astype(np.float64), axis, -1)
    blocks = v.reshape(v.shape[:-1] + (-1, 32))
    amax = np.abs(blocks).max(-1, keepdims=True)
    byte = np.maximum(np.where(amax > 0, np.frexp(amax)[1] - 1 + 127, 0) - down, 1)
    scale = np.exp2(byte - 127.0)
    codes = (blocks / scale).astype(np.float32).astype(dtype).astype(np.float64)
    return np.moveaxis((codes * scale).reshape(v.shape), -1, axis)


WIDE = False


def mx_kscale(k):
    if not WIDE:
        return np.ones(k)
    levels = np.array([10, -10, 5, -5, 0])
    if k % 512:
        return np.exp2(np.random.permutation(np.resize(levels, k // 32))).repeat(32)
    a = np.empty((k // 512, 16))
    for p in range(k // 512):
        a[p, :8] = np.random.permutation(np.resize(levels, 8))
        for g in range(8):
            far = levels[np.abs(levels - a[p, g]) >= 10]
            a[p, g + 8] = far[np.random.randint(len(far))]
    return np.exp2(a.ravel()).repeat(32)


def f64(x):
    return np.asarray(x).astype(np.float64)


def striped(idx):
    return np.tile(idx.reshape(-1, 16).T, (8, 1)).astype(np.uint16)


def unstriped(offs):
    return offs[:16].T.reshape(-1).astype(np.int64)


E2M1 = np.array([0.0, 0.5, 1.0, 1.5, 2.0, 3.0, 4.0, 6.0, -0.0, -0.5, -1.0, -1.5, -2.0, -3.0, -4.0, -6.0])


def pack_weight(w, fmt):
    k, n = w.shape
    w = f64(np.asarray(w, np.float32).astype(ml_dtypes.bfloat16)).reshape(k // 32, 32, n)
    amax = np.abs(w).max(1)
    if fmt == "e4m3":
        byte = np.frexp(amax)[1] - 1 + 127 - 7
    else:
        mant, ex = np.frexp(amax / 6.0)
        byte = np.where(mant > 0.5, ex, ex - 1) + 127
    byte = np.clip(np.where(amax > 0, byte, 1), 1, 254)
    scaled = (w * np.exp2(127.0 - byte)[:, None, :]).reshape(k, n).astype(np.float32)
    by_word = np.ascontiguousarray(scaled.reshape(k // 512, 128, 4, n).transpose(0, 1, 3, 2))
    if fmt == "e4m3":
        words = by_word.astype(ml_dtypes.float8_e4m3fn).view(np.uint8)
    else:
        c = by_word.astype(ml_dtypes.float4_e2m1fn).view(np.uint8) & 0xF
        words = (c[..., 0::2] | (c[..., 1::2] << 4)).reshape(k // 512, 128, 2 * n)
    return np.ascontiguousarray(words), np.ascontiguousarray(byte.astype(np.uint8).reshape(k // 512, 16, n))


def unpack_weight(words, scales, fmt):
    g, _, n = scales.shape
    words = np.ascontiguousarray(words).reshape(g, 128, n, -1)
    if fmt == "e4m3":
        vals = words.view(ml_dtypes.float8_e4m3fn).astype(np.float64)
    else:
        nib = np.empty((g, 128, n, 4), np.uint8)
        nib[..., 0::2] = words & 0xF
        nib[..., 1::2] = words >> 4
        vals = E2M1[nib]
    vals = vals * np.repeat(np.exp2(scales.astype(np.float64) - 127.0), 8, axis=1)[..., None]
    return vals.transpose(0, 1, 3, 2).reshape(g * 512, n)


def gelu(v):
    return 0.5 * v * (1.0 + np.tanh(np.sqrt(2.0 / np.pi) * (v + 0.044715 * v**3)))


def striped8(idx):
    return np.concatenate([v.reshape(-1, 16).T for v in idx]).astype(np.uint16)


def unstriped8(offs):
    return np.stack([offs[16 * g:16 * g + 16].T.reshape(-1) for g in range(8)]).astype(np.int64)


def put_heads(h, wgs, idx8, t2):
    r = np.arange(h.shape[0])
    page = np.zeros((h.shape[0], t2))
    page[r[:, None], idx8[r % 512 // 64]] = wgs[r // 4 % 128] * h
    return page


def bf(x):
    return np.asarray(x, np.float32).astype(ml_dtypes.bfloat16)


def planes(Y):
    n, m = Y.shape
    b = f64(bf(Y)).reshape(n // 32, 32, m)
    amax = np.abs(b).max(1)
    byte = np.clip(np.where(amax > 0, np.frexp(amax)[1] - 1 + 127 - 7, 1), 1, 254)
    codes = (b * np.exp2(127.0 - byte)[:, None, :]).reshape(n, m).astype(np.float32).astype(ml_dtypes.float8_e4m3fn).view(np.uint8)
    words = codes.reshape(n // 512, 128, 4, m).transpose(0, 1, 3, 2)
    return np.ascontiguousarray(words), np.ascontiguousarray(byte.astype(np.uint8).reshape(n // 512, 16, m))


K, T, S, T2, P, H, N = 1024, 4096, 1024, 2048, 1024, 1024, 512

def setup_inputs():
    n = np.random.standard_normal
    s = mx_kscale(K)[:, None]
    u = mx_kscale(H)[:, None]
    tab_words, tab_scales = pack_weight(n((K, T)) * s, "e4m3")
    w2_words, w2_scales = pack_weight(1.2 * n((H, N)) / np.sqrt(H) / u, "e2m1")
    w3_words, w3_scales = pack_weight(0.9 * n((K, N)) / np.sqrt(K) / s, "e4m3")
    return {
        "tab_words": tab_words, "tab_scales": tab_scales,
        "offs": striped(np.random.permutation(T)[:S]),
        "offs2": striped8(np.stack([np.random.permutation(T2)[:S] for _ in range(8)])),
        "offs3": striped(np.random.permutation(T2)[:P]),
        "w1": (n((K, H)) / np.sqrt(K) / s).astype(np.float32),
        "ref": n((H, S)).astype(np.float32),
        "wgs": np.repeat(np.random.uniform(0.5, 2.0, (8, S)), 16, axis=0).astype(np.float32),
        "chamber": n((H, P)).astype(np.float32),
        "gain": (np.exp(0.3 * n(H)) * u[:, 0]).astype(np.float32),
        "w2_words": w2_words, "w2_scales": w2_scales,
        "w3_words": w3_words, "w3_scales": w3_scales,
        "fgain": np.exp(0.8 * n(N)).astype(np.float32),
    }

def reference(tab_words, tab_scales, offs, offs2, offs3, w1, ref, wgs, chamber, gain,
              w2_words, w2_scales, w3_words, w3_scales, fgain):
    v = unpack_weight(tab_words, tab_scales, "e4m3")[:, unstriped(offs)]
    w1q = mxq(f64(w1), 0, "e4m3")
    w2 = unpack_weight(w2_words, w2_scales, "e2m1")
    w3 = unpack_weight(w3_words, w3_scales, "e4m3")
    h = np.maximum(w1q.T @ v, f64(ref))
    page = put_heads(h, f64(wgs), unstriped8(offs2), T2)
    x = page[:, unstriped(offs3)]
    z = f64(gain)[:, None] * np.tanh(x + f64(chamber))
    zq = mxq(z, 0, "e4m3")
    y = f64(fgain)[:, None] * (w2.T @ zq + w3.T @ v)
    words, scales = planes(y)
    return y, words, scales

@@ -1,0 +1,276 @@
+from contextlib import ExitStack
+
+import concourse.mybir as mybir
+
+K, T, S, T2, M, H, N = 1024, 4096, 1024, 2048, 1024, 1024, 512
+FLOPS = 2 * K * H * S + 2 * H * N * M + 2 * K * N * M
+
+F32 = mybir.dt.float32
+BF16 = mybir.dt.bfloat16
+I32 = mybir.dt.int32
+U32 = mybir.dt.uint32
+U16 = mybir.dt.uint16
+U8 = mybir.dt.uint8
+FP8X4 = mybir.dt.float8_e4m3fn_x4
+FP4X4 = mybir.dt.float4_e2m1fn_x4
+ALU = mybir.AluOpType
+ACT = mybir.ActivationFunctionType
+
+P = 128
+PACK = 4
+KP = P * PACK
+BANK = 512
+SLICES = H // P
+CHUNKS = (256, 256, 256, 128, 128)
+W3_ROW = 4
+
+
+def tile_list_nearfield_probe_features_kernel(
+    tc, tab_words, tab_scales, offs, offs2, offs3, w1, ref, wgs, chamber, gain,
+    w2_words, w2_scales, w3_words, w3_scales, fgain, out_0, out_1, out_2,
+):
+    nc = tc.nc
+    with ExitStack() as ctx:
+        keep = ctx.enter_context(tc.tile_pool(name="keep", bufs=1))
+        ring = ctx.enter_context(tc.tile_pool(name="ring", bufs=2))
+        psum = ctx.enter_context(tc.psum_pool(name="psum", bufs=1))
+
+        idx = keep.tile([P, S // 16], U16, name="idx")
+        idx2 = keep.tile([P, S // 16], U16, name="idx2")
+        idx3 = keep.tile([P, M // 16], U16, name="idx3")
+        tab_w = [keep.tile([P, T], U32, name=f"tab_w{a}", align_bytes=64) for a in range(2)]
+        tab_s = keep.tile([P, T], U8, name="tab_s", align_bytes=64)
+        v_w = [keep.tile([P, S], U32, name=f"v_w{a}", align_bytes=64) for a in range(2)]
+        v_s = keep.tile([P, S], U8, name="v_s", align_bytes=64)
+        w1_q = [[keep.tile([P, KP], U32, name=f"w1_q{a}{b}", align_bytes=64) for b in range(2)] for a in range(2)]
+        w1_s = [[keep.tile([P, KP], U8, name=f"w1_s{a}{b}", align_bytes=64) for b in range(2)] for a in range(2)]
+        wgs_t = keep.tile([P, S], F32, name="wgs_t")
+        gain_t = keep.tile([P, 2, PACK], F32, name="gain_t")
+        fgain_t = keep.tile([P, PACK], F32, name="fgain_t")
+        pages = [keep.tile([P, T2], F32, name=f"page{u}", align_bytes=64) for u in range(2)]
+        z_b = [keep.tile([P, M * PACK], BF16, name=f"z_b{b}", align_bytes=64) for b in range(2)]
+        z_q = [keep.tile([P, M], U32, name=f"z_q{b}", align_bytes=64) for b in range(2)]
+        z_s = [keep.tile([P, M], U8, name=f"z_s{b}", align_bytes=64) for b in range(2)]
+        w2_raw = keep.tile([P, 2, N], U16, name="w2_raw", align_bytes=64)
+        w2_w = keep.tile([P, 2, N], U16, name="w2_w", align_bytes=64)
+        w3_raw = keep.tile([P, 2, N], I32, name="w3_raw", align_bytes=64)
+        w3_w = keep.tile([P, 2, N], I32, name="w3_w", align_bytes=64)
+        ws_raw = keep.tile([P, 2, N], U8, name="ws_raw", align_bytes=64)
+        ws = keep.tile([P, 2, N], U8, name="ws", align_bytes=64)
+        y_q = keep.tile([P, M], U32, name="y_q", align_bytes=64)
+        y_s = keep.tile([P, M], U8, name="y_s", align_bytes=64)
+
+        ref_rows = ref.rearrange("(b p i) j -> b i p j", b=2, i=PACK)
+        chamber_rows = chamber.rearrange("(b p i) j -> b i p j", b=2, i=PACK)
+        ref_t, chamber_t, h_t, w1_raw = {}, {}, {}, {}
+
+        def load_ref(s):
+            ref_t[s] = ring.tile([P, S], F32, name="ref_t", bufs=4)
+            nc.sync.dma_start(ref_t[s][:], ref_rows[s // PACK, s % PACK])
+
+        def load_chamber(s):
+            chamber_t[s] = ring.tile([P, M], F32, name="chamber_t", bufs=4)
+            nc.sync.dma_start(chamber_t[s][:], chamber_rows[s // PACK, s % PACK])
+
+        def load_w1(a, b):
+            w1_raw[a, b] = ring.tile([P, PACK, KP], F32, name="w1_raw", bufs=3)
+            rows = w1[a * KP : (a + 1) * KP, b * KP : (b + 1) * KP]
+            nc.sync.dma_start(w1_raw[a, b][:], rows.rearrange("(p j) c -> p j c", j=PACK))
+
+        def load_tab(a):
+            nc.sync.dma_start(tab_w[a][:].bitcast(I32), tab_words[a].rearrange("p t i -> p (t i)").bitcast(I32))
+
+        def quantise_w1(a, b):
+            grouped = ring.tile([P, KP * PACK], BF16, name="w1_grouped", align_bytes=64)
+            nc.scalar.copy(
+                grouped[:].rearrange("p (i q j) -> p i q j", i=PACK, j=PACK),
+                w1_raw[a, b][:].rearrange("p j (q i) -> p i q j", i=PACK),
+            )
+            nc.vector.quantize_mx(w1_q[a][b][:].bitcast(FP8X4), w1_s[a][b][:], grouped[:])
+
+        def gather_words(a, lo, hi):
+            nc.vector.tensor_copy(v_w[a][:, lo:hi], tab_w[a][:].indirect(idx[:, lo // 16 : hi // 16]))
+
+        def port_features(s):
+            b, i = divmod(s, PACK)
+            cols = slice(i * P, (i + 1) * P)
+            h_t[s] = ring.tile([P, S], F32, name="h_t")
+            for half in range(2):
+                j = slice(half * BANK, (half + 1) * BANK)
+                acc = psum.tile([P, BANK], F32, name=f"bank{6 + half}")
+                for a in range(2):
+                    nc.tensor.matmul_mx(
+                        acc[:], lhsT=w1_q[a][b][:, cols].bitcast(FP8X4), lhsT_scale=w1_s[a][b][:, cols],
+                        rhs=v_w[a][:, j].bitcast(FP8X4), rhs_scale=v_s[4 * a : P, j], start=(a == 0), stop=(a == 1),
+                    )
+                nc.vector.tensor_tensor(h_t[s][:, j], acc[:], ref_t[s][:, j], ALU.max)
+
+        def put(s):
+            nc.vector.tensor_tensor(pages[s % 2][:].indirect(idx2[:]), h_t[s][:], wgs_t[:], ALU.mult)
+
+        def fetch(s, x, lo, hi):
+            nc.vector.tensor_tensor(
+                x[:, lo:hi], pages[s % 2][:].indirect(idx3[:, lo // 16 : hi // 16]), chamber_t[s][:, lo:hi], ALU.add
+            )
+
+        def angle_features(s, x, lo, hi):
+            b, i = divmod(s, PACK)
+            nc.scalar.activation(x[:, lo:hi], x[:, lo:hi], ACT.Tanh)
+            z_plane = z_b[b][:].rearrange("p (m i) -> p m i", i=PACK)[:, lo:hi, i]
+            nc.scalar.activation(z_plane, x[:, lo:hi], ACT.Copy, scale=gain_t[:, b, i : i + 1])
+
+        def quantise_z(b, lo, hi):
+            nc.vector.quantize_mx(z_q[b][:, lo:hi].bitcast(FP8X4), z_s[b][:, lo:hi], z_b[b][:, PACK * lo : PACK * hi])
+
+        def deal(dst, src, run):
+            for a in range(2):
+                nc.vector.tensor_copy(
+                    dst[:, a, :].rearrange("p (t c i) -> p c t i", t=PACK, i=run),
+                    src[:, a, :].rearrange("p (c i t) -> p c t i", t=PACK, i=run),
+                )
+
+        nc.vector.memset(tab_s[:].bitcast(I32), 0)
+        for q in range(4):
+            nc.scalar.dma_start(
+                tab_s[32 * q : 32 * q + 8, :].bitcast(I32), tab_scales[:, 4 * q : 4 * q + 4, :].bitcast(I32)
+            )
+        nc.vector.memset(ws_raw[:].rearrange("p a n -> p (a n)").bitcast(I32), 0)
+        for page in pages:
+            nc.vector.memset(page[:], 0.0)
+        load_w1(0, 0)
+        nc.sync.dma_start(idx[:], offs)
+        nc.sync.dma_start(idx2[:], offs2)
+        nc.sync.dma_start(idx3[:], offs3)
+        nc.sync.dma_start(gain_t[:], gain.rearrange("(b p i) -> p b i", b=2, i=PACK))
+        load_tab(0)
+        load_w1(1, 0)
+        load_tab(1)
+        load_ref(0)
+        nc.sync.dma_start(wgs_t[:], wgs)
+        load_ref(1)
+        load_chamber(0)
+        load_ref(2)
+        load_chamber(1)
+        load_w1(0, 1)
+        load_ref(3)
+        load_chamber(2)
+
+        quantise_w1(0, 0)
+        gather_words(0, 0, S)
+        quantise_w1(1, 0)
+        nc.vector.tensor_copy(v_s[:], tab_s[:].indirect(idx[:]))
+        gather_words(1, 0, BANK)
+        gather_words(1, BANK, S)
+
+        load_w1(1, 1)
+        load_chamber(3)
+        nc.sync.dma_start(w3_raw[:], w3_words.rearrange("a p c i -> p a (c i)").bitcast(I32))
+        nc.sync.dma_start(w2_raw[:].bitcast(I32), w2_words.rearrange("a p c -> p a c").bitcast(I32))
+        for row, scales in ((0, w2_scales), (W3_ROW, w3_scales)):
+            for q in range(4):
+                nc.sync.dma_start(
+                    ws_raw[32 * q + row : 32 * q + row + 4].bitcast(I32),
+                    scales[:, 4 * q : 4 * q + 4, :].rearrange("a r n -> r a n").bitcast(I32),
+                )
+        nc.sync.dma_start(fgain_t[:], fgain.rearrange("(p t) -> p t", t=PACK))
+
+        starts = [sum(CHUNKS[:c]) for c in range(len(CHUNKS))]
+        sums = {}
+        first_bank = [sum(PACK * w // BANK for w in CHUNKS[:c]) for c in range(len(CHUNKS))]
+
+        def far_pass(c, t, kind, a, start=False, stop=False):
+            m = slice(starts[c], starts[c] + CHUNKS[c])
+            n = slice(t * P, (t + 1) * P)
+            if kind == "w3":
+                nc.tensor.matmul_mx(
+                    sums[c, t], lhsT=w3_w[:, a, n].bitcast(FP8X4), lhsT_scale=ws[W3_ROW:P, a, n],
+                    rhs=v_w[a][:, m].bitcast(FP8X4), rhs_scale=v_s[4 * a : P, m], start=start, stop=stop,
+                )
+            else:
+                nc.tensor.matmul_mx(
+                    sums[c, t], lhsT=w2_w[:, a, n].bitcast(FP4X4), lhsT_scale=ws[:, a, n],
+                    rhs=z_q[a][:, m].bitcast(FP8X4), rhs_scale=z_s[a][:, m], start=start, stop=stop,
+                )
+
+        def far_early(c):
+            per_bank = BANK // CHUNKS[c]
+            for t in range(PACK):
+                if t % per_bank == 0:
+                    bank = psum.tile([P, BANK], F32, name=f"bank{first_bank[c] + t // per_bank}")
+                sums[c, t] = bank[:, (t % per_bank) * CHUNKS[c] : (t % per_bank + 1) * CHUNKS[c]]
+                far_pass(c, t, "w3", 0, start=(t % per_bank == 0))
+                far_pass(c, t, "w3", 1)
+                far_pass(c, t, "w2", 0)
+
+        def far_last(c):
+            per_bank = BANK // CHUNKS[c]
+            for t in range(PACK):
+                far_pass(c, t, "w2", 1, stop=(t % per_bank == per_bank - 1))
+
+        y_f = {}
+
+        def far_out(c):
+            w = CHUNKS[c]
+            y_f[c] = keep.tile([P, PACK, w], F32, name=f"y_f{c}", align_bytes=64)
+            for t in range(PACK):
+                nc.scalar.activation(y_f[c][:, t, :], sums[c, t], ACT.Copy, scale=fgain_t[:, t : t + 1])
+            nc.sync.dma_start(
+                out_0.rearrange("(p t) m -> p t m", t=PACK)[:, :, starts[c] : starts[c] + w], y_f[c][:]
+            )
+
+        def far_planes(c):
+            w = CHUNKS[c]
+            m = slice(starts[c], starts[c] + w)
+            y_b = ring.tile([P, PACK * w], BF16, name="y_b", align_bytes=64)
+            nc.vector.tensor_copy(
+                y_b[:].rearrange("p (c i t) -> p c t i", i=4, t=PACK),
+                y_f[c][:].rearrange("p t (c i) -> p c t i", i=4),
+            )
+            nc.vector.quantize_mx(y_q[:, m].bitcast(FP8X4), y_s[:, m], y_b[:])
+            nc.sync.dma_start(out_1[0].rearrange("p m t -> p (m t)").bitcast(I32)[:, m], y_q[:, m].bitcast(I32))
+
+        port_features(0)
+        put(0)
+        for s in range(1, SLICES):
+            if s + 3 < SLICES:
+                load_ref(s + 3)
+            if s == 2:
+                quantise_w1(0, 1)
+            if s == 3:
+                quantise_w1(1, 1)
+            port_features(s)
+            x = ring.tile([P, M], F32, name="x", bufs=3)
+            fetch(s - 1, x, 0, M)
+            if s + 3 < SLICES:
+                load_chamber(s + 3)
+            angle_features(s - 1, x, 0, M)
+            if s == 5:
+                quantise_z(0, 0, M)
+                deal(w3_w, w3_raw, 4)
+            if s == 6:
+                deal(w2_w, w2_raw, 8)
+                deal(ws, ws_raw, 16)
+            put(s)
+        for c in range(len(CHUNKS)):
+            far_early(c)
+
+        last = SLICES - 1
+        x = ring.tile([P, M], F32, name="x", bufs=3)
+        n_chunks = len(CHUNKS)
+        for step in range(n_chunks + 3):
+            if step < n_chunks:
+                lo, hi = starts[step], starts[step] + CHUNKS[step]
+                fetch(last, x, lo, hi)
+                angle_features(last, x, lo, hi)
+            c = step - 1
+            if 0 <= c < n_chunks:
+                quantise_z(1, starts[c], starts[c] + CHUNKS[c])
+                far_last(c)
+            c = step - 2
+            if 0 <= c < n_chunks:
+                far_out(c)
+            c = step - 3
+            if 0 <= c < n_chunks:
+                far_planes(c)
+        for q in range(4):
+            nc.scalar.dma_start(out_2[0, 4 * q : 4 * q + 4, :].bitcast(I32), y_s[32 * q : 32 * q + 4, :].bitcast(I32))

@@ -21,7 +21,7 @@ PACK = 4
 KP = P * PACK
 BANK = 512
 SLICES = H // P
-CHUNKS = (256, 256, 256, 128, 128)
+CHUNKS = (128, 256, 256, 256, 128)
 W3_ROW = 4
 
 
@@ -113,52 +113,54 @@ def tile_list_nearfield_probe_features_kernel(
                 x[:, lo:hi], pages[s % 2][:].indirect(idx3[:, lo // 16 : hi // 16]), chamber_t[s][:, lo:hi], ALU.add
             )
 
-        def angle_features(s, x, lo, hi):
+        def angle_features(s, x, lo, hi, on_vector=False):
             b, i = divmod(s, PACK)
             nc.scalar.activation(x[:, lo:hi], x[:, lo:hi], ACT.Tanh)
             z_plane = z_b[b][:].rearrange("p (m i) -> p m i", i=PACK)[:, lo:hi, i]
-            nc.scalar.activation(z_plane, x[:, lo:hi], ACT.Copy, scale=gain_t[:, b, i : i + 1])
+            if on_vector:
+                nc.vector.tensor_scalar(z_plane, x[:, lo:hi], gain_t[:, b, i : i + 1], None, ALU.mult)
+            else:
+                nc.scalar.activation(z_plane, x[:, lo:hi], ACT.Copy, scale=gain_t[:, b, i : i + 1])
 
         def quantise_z(b, lo, hi):
             nc.vector.quantize_mx(z_q[b][:, lo:hi].bitcast(FP8X4), z_s[b][:, lo:hi], z_b[b][:, PACK * lo : PACK * hi])
 
         def deal(dst, src, run):
-            for a in range(2):
-                nc.vector.tensor_copy(
-                    dst[:, a, :].rearrange("p (t c i) -> p c t i", t=PACK, i=run),
-                    src[:, a, :].rearrange("p (c i t) -> p c t i", t=PACK, i=run),
-                )
+            nc.vector.tensor_copy(
+                dst[:].rearrange("p a (t c i) -> p a c t i", t=PACK, i=run),
+                src[:].rearrange("p a (c i t) -> p a c t i", t=PACK, i=run),
+            )
 
         nc.vector.memset(tab_s[:].bitcast(I32), 0)
+        load_w1(0, 0)
         for q in range(4):
-            nc.scalar.dma_start(
+            nc.sync.dma_start(
                 tab_s[32 * q : 32 * q + 8, :].bitcast(I32), tab_scales[:, 4 * q : 4 * q + 4, :].bitcast(I32)
             )
         nc.vector.memset(ws_raw[:].rearrange("p a n -> p (a n)").bitcast(I32), 0)
         for page in pages:
             nc.vector.memset(page[:], 0.0)
-        load_w1(0, 0)
         nc.sync.dma_start(idx[:], offs)
-        nc.sync.dma_start(idx2[:], offs2)
-        nc.sync.dma_start(idx3[:], offs3)
-        nc.sync.dma_start(gain_t[:], gain.rearrange("(b p i) -> p b i", b=2, i=PACK))
-        load_tab(0)
         load_w1(1, 0)
+        load_tab(0)
         load_tab(1)
         load_ref(0)
         nc.sync.dma_start(wgs_t[:], wgs)
+        nc.sync.dma_start(idx2[:], offs2)
+        nc.sync.dma_start(idx3[:], offs3)
         load_ref(1)
         load_chamber(0)
+        nc.sync.dma_start(gain_t[:], gain.rearrange("(b p i) -> p b i", b=2, i=PACK))
         load_ref(2)
         load_chamber(1)
         load_w1(0, 1)
         load_ref(3)
         load_chamber(2)
 
+        nc.vector.tensor_copy(v_s[:], tab_s[:].indirect(idx[:]))
         quantise_w1(0, 0)
         gather_words(0, 0, S)
         quantise_w1(1, 0)
-        nc.vector.tensor_copy(v_s[:], tab_s[:].indirect(idx[:]))
         gather_words(1, 0, BANK)
         gather_words(1, BANK, S)
 
@@ -261,7 +263,7 @@ def tile_list_nearfield_probe_features_kernel(
             if step < n_chunks:
                 lo, hi = starts[step], starts[step] + CHUNKS[step]
                 fetch(last, x, lo, hi)
-                angle_features(last, x, lo, hi)
+                angle_features(last, x, lo, hi, on_vector=step >= 2)
             c = step - 1
             if 0 <= c < n_chunks:
                 quantise_z(1, starts[c], starts[c] + CHUNKS[c])

@@ -1,6 +1,7 @@
 from contextlib import ExitStack
 
 import concourse.mybir as mybir
+from concourse.masks import make_identity
 
 K, T, S, T2, M, H, N = 1024, 4096, 1024, 2048, 1024, 1024, 512
 FLOPS = 2 * K * H * S + 2 * H * N * M + 2 * K * N * M
@@ -91,19 +92,25 @@ def tile_list_nearfield_probe_features_kernel(
         def gather_words(a, lo, hi):
             nc.vector.tensor_copy(v_w[a][:, lo:hi], tab_w[a][:].indirect(idx[:, lo // 16 : hi // 16]))
 
-        def port_features(s):
+        acc = {}
+
+        def first_product(s):
             b, i = divmod(s, PACK)
             cols = slice(i * P, (i + 1) * P)
+            for half in range(2):
+                j = slice(half * BANK, (half + 1) * BANK)
+                acc[s, half] = psum.tile([P, BANK], F32, name=f"bank{3 + half}")
+                for a in range(2):
+                    nc.tensor.matmul_mx(
+                        acc[s, half][:], lhsT=w1_q[a][b][:, cols].bitcast(FP8X4), lhsT_scale=w1_s[a][b][:, cols],
+                        rhs=v_w[a][:, j].bitcast(FP8X4), rhs_scale=v_s[4 * a : P, j], start=(a == 0), stop=(a == 1),
+                    )
+
+        def port_features(s):
             h_t[s] = ring.tile([P, S], F32, name="h_t")
             for half in range(2):
                 j = slice(half * BANK, (half + 1) * BANK)
-                acc = psum.tile([P, BANK], F32, name=f"bank{6 + half}")
-                for a in range(2):
-                    nc.tensor.matmul_mx(
-                        acc[:], lhsT=w1_q[a][b][:, cols].bitcast(FP8X4), lhsT_scale=w1_s[a][b][:, cols],
-                        rhs=v_w[a][:, j].bitcast(FP8X4), rhs_scale=v_s[4 * a : P, j], start=(a == 0), stop=(a == 1),
-                    )
-                nc.vector.tensor_tensor(h_t[s][:, j], acc[:], ref_t[s][:, j], ALU.max)
+                nc.vector.tensor_tensor(h_t[s][:, j], acc[s, half][:], ref_t[s][:, j], ALU.max)
 
         def put(s):
             nc.vector.tensor_tensor(pages[s % 2][:].indirect(idx2[:]), h_t[s][:], wgs_t[:], ALU.mult)
@@ -122,6 +129,28 @@ def tile_list_nearfield_probe_features_kernel(
             else:
                 nc.scalar.activation(z_plane, x[:, lo:hi], ACT.Copy, scale=gain_t[:, b, i : i + 1])
 
+        def fetch_plain(s, x):
+            nc.vector.tensor_copy(x[:], pages[s % 2][:].indirect(idx3[:]))
+
+        def angle_features_turned(s, x):
+            b, i = divmod(s, PACK)
+            bent = []
+            for half in range(2):
+                turned = psum.tile([P, BANK], F32, name=f"bank{5 + half}")
+                for u in range(BANK // P):
+                    m = slice(half * BANK + u * P, half * BANK + (u + 1) * P)
+                    block = turned[:, u * P : (u + 1) * P]
+                    nc.tensor.matmul(block, chamber_t[s][:, m], ident[:], start=True, stop=False, is_transpose=True)
+                    nc.tensor.matmul(block, x[:, m], ident[:], start=False, stop=True, is_transpose=True)
+                bent.append(ring.tile([P, BANK], F32, name="bent"))
+                nc.scalar.activation(bent[half][:], turned[:], ACT.Tanh)
+            for half in range(2):
+                back = psum.tile([P, BANK], F32, name=f"bank{5 + half}")
+                for u in range(BANK // P):
+                    nc.tensor.transpose(back[:, u * P : (u + 1) * P], bent[half][:, u * P : (u + 1) * P], ident[:])
+                z_plane = z_b[b][:].rearrange("p (m i) -> p m i", i=PACK)[:, half * BANK : (half + 1) * BANK, i]
+                nc.scalar.activation(z_plane, back[:], ACT.Copy, scale=gain_t[:, b, i : i + 1])
+
         def quantise_z(b, lo, hi):
             nc.vector.quantize_mx(z_q[b][:, lo:hi].bitcast(FP8X4), z_s[b][:, lo:hi], z_b[b][:, PACK * lo : PACK * hi])
 
@@ -131,6 +160,8 @@ def tile_list_nearfield_probe_features_kernel(
                 src[:].rearrange("p a (c i t) -> p a c t i", t=PACK, i=run),
             )
 
+        ident = keep.tile([P, P], F32, name="ident")
+        make_identity(nc, ident[:])
         nc.vector.memset(tab_s[:].bitcast(I32), 0)
         load_w1(0, 0)
         for q in range(4):
@@ -149,13 +180,7 @@ def tile_list_nearfield_probe_features_kernel(
         nc.sync.dma_start(idx2[:], offs2)
         nc.sync.dma_start(idx3[:], offs3)
         load_ref(1)
-        load_chamber(0)
-        nc.sync.dma_start(gain_t[:], gain.rearrange("(b p i) -> p b i", b=2, i=PACK))
-        load_ref(2)
-        load_chamber(1)
         load_w1(0, 1)
-        load_ref(3)
-        load_chamber(2)
 
         nc.vector.tensor_copy(v_s[:], tab_s[:].indirect(idx[:]))
         quantise_w1(0, 0)
@@ -165,6 +190,11 @@ def tile_list_nearfield_probe_features_kernel(
         gather_words(1, BANK, S)
 
         load_w1(1, 1)
+        load_chamber(0)
+        nc.sync.dma_start(gain_t[:], gain.rearrange("(b p i) -> p b i", b=2, i=PACK))
+        for s in range(1, 3):
+            load_ref(s + 1)
+            load_chamber(s)
         load_chamber(3)
         nc.sync.dma_start(w3_raw[:], w3_words.rearrange("a p c i -> p a (c i)").bitcast(I32))
         nc.sync.dma_start(w2_raw[:].bitcast(I32), w2_words.rearrange("a p c -> p a c").bitcast(I32))
@@ -231,21 +261,26 @@ def tile_list_nearfield_probe_features_kernel(
             nc.vector.quantize_mx(y_q[:, m].bitcast(FP8X4), y_s[:, m], y_b[:])
             nc.sync.dma_start(out_1[0].rearrange("p m t -> p (m t)").bitcast(I32)[:, m], y_q[:, m].bitcast(I32))
 
+        first_product(0)
         port_features(0)
+        first_product(1)
         put(0)
+        quantise_w1(0, 1)
+        quantise_w1(1, 1)
         for s in range(1, SLICES):
             if s + 3 < SLICES:
                 load_ref(s + 3)
-            if s == 2:
-                quantise_w1(0, 1)
-            if s == 3:
-                quantise_w1(1, 1)
             port_features(s)
             x = ring.tile([P, M], F32, name="x", bufs=3)
-            fetch(s - 1, x, 0, M)
+            if s < SLICES - 1:
+                fetch_plain(s - 1, x)
+                first_product(s + 1)
+                angle_features_turned(s - 1, x)
+            else:
+                fetch(s - 1, x, 0, M)
+                angle_features(s - 1, x, 0, M)
             if s + 3 < SLICES:
                 load_chamber(s + 3)
-            angle_features(s - 1, x, 0, M)
             if s == 5:
                 quantise_z(0, 0, M)
                 deal(w3_w, w3_raw, 4)

from contextlib import ExitStack

import concourse.mybir as mybir
from concourse.masks import make_identity

K, T, S, T2, M, H, N = 1024, 4096, 1024, 2048, 1024, 1024, 512
FLOPS = 2 * K * H * S + 2 * H * N * M + 2 * K * N * M

F32 = mybir.dt.float32
BF16 = mybir.dt.bfloat16
I32 = mybir.dt.int32
U32 = mybir.dt.uint32
U16 = mybir.dt.uint16
U8 = mybir.dt.uint8
FP8X4 = mybir.dt.float8_e4m3fn_x4
FP4X4 = mybir.dt.float4_e2m1fn_x4
ALU = mybir.AluOpType
ACT = mybir.ActivationFunctionType

P = 128
PACK = 4
KP = P * PACK
BANK = 512
SLICES = H // P
CHUNKS = (128, 256, 256, 256, 128)
W3_ROW = 4


def tile_list_nearfield_probe_features_kernel(
    tc, tab_words, tab_scales, offs, offs2, offs3, w1, ref, wgs, chamber, gain,
    w2_words, w2_scales, w3_words, w3_scales, fgain, out_0, out_1, out_2,
):
    nc = tc.nc
    with ExitStack() as ctx:
        keep = ctx.enter_context(tc.tile_pool(name="keep", bufs=1))
        ring = ctx.enter_context(tc.tile_pool(name="ring", bufs=2))
        psum = ctx.enter_context(tc.psum_pool(name="psum", bufs=1))

        idx = keep.tile([P, S // 16], U16, name="idx")
        idx2 = keep.tile([P, S // 16], U16, name="idx2")
        idx3 = keep.tile([P, M // 16], U16, name="idx3")
        tab_w = [keep.tile([P, T], U32, name=f"tab_w{a}", align_bytes=64) for a in range(2)]
        tab_s = keep.tile([P, T], U8, name="tab_s", align_bytes=64)
        v_w = [keep.tile([P, S], U32, name=f"v_w{a}", align_bytes=64) for a in range(2)]
        v_s = keep.tile([P, S], U8, name="v_s", align_bytes=64)
        w1_q = [[keep.tile([P, KP], U32, name=f"w1_q{a}{b}", align_bytes=64) for b in range(2)] for a in range(2)]
        w1_s = [[keep.tile([P, KP], U8, name=f"w1_s{a}{b}", align_bytes=64) for b in range(2)] for a in range(2)]
        wgs_t = keep.tile([P, S], F32, name="wgs_t")
        gain_t = keep.tile([P, 2, PACK], F32, name="gain_t")
        fgain_t = keep.tile([P, PACK], F32, name="fgain_t")
        pages = [keep.tile([P, T2], F32, name=f"page{u}", align_bytes=64) for u in range(2)]
        z_b = [keep.tile([P, M * PACK], BF16, name=f"z_b{b}", align_bytes=64) for b in range(2)]
        z_q = [keep.tile([P, M], U32, name=f"z_q{b}", align_bytes=64) for b in range(2)]
        z_s = [keep.tile([P, M], U8, name=f"z_s{b}", align_bytes=64) for b in range(2)]
        w2_raw = keep.tile([P, 2, N], U16, name="w2_raw", align_bytes=64)
        w2_w = keep.tile([P, 2, N], U16, name="w2_w", align_bytes=64)
        w3_raw = keep.tile([P, 2, N], I32, name="w3_raw", align_bytes=64)
        w3_w = keep.tile([P, 2, N], I32, name="w3_w", align_bytes=64)
        ws_raw = keep.tile([P, 2, N], U8, name="ws_raw", align_bytes=64)
        ws = keep.tile([P, 2, N], U8, name="ws", align_bytes=64)
        y_q = keep.tile([P, M], U32, name="y_q", align_bytes=64)
        y_s = keep.tile([P, M], U8, name="y_s", align_bytes=64)

        ref_rows = ref.rearrange("(b p i) j -> b i p j", b=2, i=PACK)
        chamber_rows = chamber.rearrange("(b p i) j -> b i p j", b=2, i=PACK)
        ref_t, chamber_t, h_t, w1_raw = {}, {}, {}, {}

        def load_ref(s):
            ref_t[s] = ring.tile([P, S], F32, name="ref_t", bufs=4)
            nc.sync.dma_start(ref_t[s][:], ref_rows[s // PACK, s % PACK])

        def load_chamber(s):
            chamber_t[s] = ring.tile([P, M], F32, name="chamber_t", bufs=4)
            nc.sync.dma_start(chamber_t[s][:], chamber_rows[s // PACK, s % PACK])

        def load_w1(a, b):
            w1_raw[a, b] = ring.tile([P, PACK, KP], F32, name="w1_raw", bufs=3)
            rows = w1[a * KP : (a + 1) * KP, b * KP : (b + 1) * KP]
            nc.sync.dma_start(w1_raw[a, b][:], rows.rearrange("(p j) c -> p j c", j=PACK))

        def load_tab(a):
            nc.sync.dma_start(tab_w[a][:].bitcast(I32), tab_words[a].rearrange("p t i -> p (t i)").bitcast(I32))

        def quantise_w1(a, b):
            grouped = ring.tile([P, KP * PACK], BF16, name="w1_grouped", align_bytes=64)
            nc.scalar.copy(
                grouped[:].rearrange("p (i q j) -> p i q j", i=PACK, j=PACK),
                w1_raw[a, b][:].rearrange("p j (q i) -> p i q j", i=PACK),
            )
            nc.vector.quantize_mx(w1_q[a][b][:].bitcast(FP8X4), w1_s[a][b][:], grouped[:])

        def gather_words(a, lo, hi):
            nc.vector.tensor_copy(v_w[a][:, lo:hi], tab_w[a][:].indirect(idx[:, lo // 16 : hi // 16]))

        acc = {}

        def first_product(s):
            b, i = divmod(s, PACK)
            cols = slice(i * P, (i + 1) * P)
            for half in range(2):
                j = slice(half * BANK, (half + 1) * BANK)
                acc[s, half] = psum.tile([P, BANK], F32, name=f"bank{3 + half}")
                for a in range(2):
                    nc.tensor.matmul_mx(
                        acc[s, half][:], lhsT=w1_q[a][b][:, cols].bitcast(FP8X4), lhsT_scale=w1_s[a][b][:, cols],
                        rhs=v_w[a][:, j].bitcast(FP8X4), rhs_scale=v_s[4 * a : P, j], start=(a == 0), stop=(a == 1),
                    )

        def port_features(s):
            h_t[s] = ring.tile([P, S], F32, name="h_t")
            for half in range(2):
                j = slice(half * BANK, (half + 1) * BANK)
                nc.vector.tensor_tensor(h_t[s][:, j], acc[s, half][:], ref_t[s][:, j], ALU.max)

        def put(s):
            nc.vector.tensor_tensor(pages[s % 2][:].indirect(idx2[:]), h_t[s][:], wgs_t[:], ALU.mult)

        def fetch(s, x, lo, hi):
            nc.vector.tensor_tensor(
                x[:, lo:hi], pages[s % 2][:].indirect(idx3[:, lo // 16 : hi // 16]), chamber_t[s][:, lo:hi], ALU.add
            )

        def angle_features(s, x, lo, hi, on_vector=False):
            b, i = divmod(s, PACK)
            nc.scalar.activation(x[:, lo:hi], x[:, lo:hi], ACT.Tanh)
            z_plane = z_b[b][:].rearrange("p (m i) -> p m i", i=PACK)[:, lo:hi, i]
            if on_vector:
                nc.vector.tensor_scalar(z_plane, x[:, lo:hi], gain_t[:, b, i : i + 1], None, ALU.mult)
            else:
                nc.scalar.activation(z_plane, x[:, lo:hi], ACT.Copy, scale=gain_t[:, b, i : i + 1])

        def fetch_plain(s, x):
            nc.vector.tensor_copy(x[:], pages[s % 2][:].indirect(idx3[:]))

        def angle_features_turned(s, x):
            b, i = divmod(s, PACK)
            bent = []
            for half in range(2):
                turned = psum.tile([P, BANK], F32, name=f"bank{5 + half}")
                for u in range(BANK // P):
                    m = slice(half * BANK + u * P, half * BANK + (u + 1) * P)
                    block = turned[:, u * P : (u + 1) * P]
                    nc.tensor.matmul(block, chamber_t[s][:, m], ident[:], start=True, stop=False, is_transpose=True)
                    nc.tensor.matmul(block, x[:, m], ident[:], start=False, stop=True, is_transpose=True)
                bent.append(ring.tile([P, BANK], F32, name="bent"))
                nc.scalar.activation(bent[half][:], turned[:], ACT.Tanh)
            for half in range(2):
                back = psum.tile([P, BANK], F32, name=f"bank{5 + half}")
                for u in range(BANK // P):
                    nc.tensor.transpose(back[:, u * P : (u + 1) * P], bent[half][:, u * P : (u + 1) * P], ident[:])
                z_plane = z_b[b][:].rearrange("p (m i) -> p m i", i=PACK)[:, half * BANK : (half + 1) * BANK, i]
                nc.scalar.activation(z_plane, back[:], ACT.Copy, scale=gain_t[:, b, i : i + 1])

        def quantise_z(b, lo, hi):
            nc.vector.quantize_mx(z_q[b][:, lo:hi].bitcast(FP8X4), z_s[b][:, lo:hi], z_b[b][:, PACK * lo : PACK * hi])

        def deal(dst, src, run):
            nc.vector.tensor_copy(
                dst[:].rearrange("p a (t c i) -> p a c t i", t=PACK, i=run),
                src[:].rearrange("p a (c i t) -> p a c t i", t=PACK, i=run),
            )

        ident = keep.tile([P, P], F32, name="ident")
        make_identity(nc, ident[:])
        nc.vector.memset(tab_s[:].bitcast(I32), 0)
        load_w1(0, 0)
        for q in range(4):
            nc.sync.dma_start(
                tab_s[32 * q : 32 * q + 8, :].bitcast(I32), tab_scales[:, 4 * q : 4 * q + 4, :].bitcast(I32)
            )
        nc.vector.memset(ws_raw[:].rearrange("p a n -> p (a n)").bitcast(I32), 0)
        for page in pages:
            nc.vector.memset(page[:], 0.0)
        nc.sync.dma_start(idx[:], offs)
        load_w1(1, 0)
        load_tab(0)
        load_tab(1)
        load_ref(0)
        nc.sync.dma_start(wgs_t[:], wgs)
        nc.sync.dma_start(idx2[:], offs2)
        nc.sync.dma_start(idx3[:], offs3)
        load_ref(1)
        load_w1(0, 1)

        nc.vector.tensor_copy(v_s[:], tab_s[:].indirect(idx[:]))
        quantise_w1(0, 0)
        gather_words(0, 0, S)
        quantise_w1(1, 0)
        gather_words(1, 0, BANK)
        gather_words(1, BANK, S)

        load_w1(1, 1)
        load_chamber(0)
        nc.sync.dma_start(gain_t[:], gain.rearrange("(b p i) -> p b i", b=2, i=PACK))
        for s in range(1, 3):
            load_ref(s + 1)
            load_chamber(s)
        load_chamber(3)
        nc.sync.dma_start(w3_raw[:], w3_words.rearrange("a p c i -> p a (c i)").bitcast(I32))
        nc.sync.dma_start(w2_raw[:].bitcast(I32), w2_words.rearrange("a p c -> p a c").bitcast(I32))
        for row, scales in ((0, w2_scales), (W3_ROW, w3_scales)):
            for q in range(4):
                nc.sync.dma_start(
                    ws_raw[32 * q + row : 32 * q + row + 4].bitcast(I32),
                    scales[:, 4 * q : 4 * q + 4, :].rearrange("a r n -> r a n").bitcast(I32),
                )
        nc.sync.dma_start(fgain_t[:], fgain.rearrange("(p t) -> p t", t=PACK))

        starts = [sum(CHUNKS[:c]) for c in range(len(CHUNKS))]
        sums = {}
        first_bank = [sum(PACK * w // BANK for w in CHUNKS[:c]) for c in range(len(CHUNKS))]

        def far_pass(c, t, kind, a, start=False, stop=False):
            m = slice(starts[c], starts[c] + CHUNKS[c])
            n = slice(t * P, (t + 1) * P)
            if kind == "w3":
                nc.tensor.matmul_mx(
                    sums[c, t], lhsT=w3_w[:, a, n].bitcast(FP8X4), lhsT_scale=ws[W3_ROW:P, a, n],
                    rhs=v_w[a][:, m].bitcast(FP8X4), rhs_scale=v_s[4 * a : P, m], start=start, stop=stop,
                )
            else:
                nc.tensor.matmul_mx(
                    sums[c, t], lhsT=w2_w[:, a, n].bitcast(FP4X4), lhsT_scale=ws[:, a, n],
                    rhs=z_q[a][:, m].bitcast(FP8X4), rhs_scale=z_s[a][:, m], start=start, stop=stop,
                )

        def far_early(c):
            per_bank = BANK // CHUNKS[c]
            for t in range(PACK):
                if t % per_bank == 0:
                    bank = psum.tile([P, BANK], F32, name=f"bank{first_bank[c] + t // per_bank}")
                sums[c, t] = bank[:, (t % per_bank) * CHUNKS[c] : (t % per_bank + 1) * CHUNKS[c]]
                far_pass(c, t, "w3", 0, start=(t % per_bank == 0))
                far_pass(c, t, "w3", 1)
                far_pass(c, t, "w2", 0)

        def far_last(c):
            per_bank = BANK // CHUNKS[c]
            for t in range(PACK):
                far_pass(c, t, "w2", 1, stop=(t % per_bank == per_bank - 1))

        y_f = {}

        def far_out(c):
            w = CHUNKS[c]
            y_f[c] = keep.tile([P, PACK, w], F32, name=f"y_f{c}", align_bytes=64)
            for t in range(PACK):
                nc.scalar.activation(y_f[c][:, t, :], sums[c, t], ACT.Copy, scale=fgain_t[:, t : t + 1])
            nc.sync.dma_start(
                out_0.rearrange("(p t) m -> p t m", t=PACK)[:, :, starts[c] : starts[c] + w], y_f[c][:]
            )

        def far_planes(c):
            w = CHUNKS[c]
            m = slice(starts[c], starts[c] + w)
            y_b = ring.tile([P, PACK * w], BF16, name="y_b", align_bytes=64)
            nc.vector.tensor_copy(
                y_b[:].rearrange("p (c i t) -> p c t i", i=4, t=PACK),
                y_f[c][:].rearrange("p t (c i) -> p c t i", i=4),
            )
            nc.vector.quantize_mx(y_q[:, m].bitcast(FP8X4), y_s[:, m], y_b[:])
            nc.sync.dma_start(out_1[0].rearrange("p m t -> p (m t)").bitcast(I32)[:, m], y_q[:, m].bitcast(I32))

        first_product(0)
        port_features(0)
        first_product(1)
        put(0)
        quantise_w1(0, 1)
        quantise_w1(1, 1)
        for s in range(1, SLICES):
            if s + 3 < SLICES:
                load_ref(s + 3)
            port_features(s)
            x = ring.tile([P, M], F32, name="x", bufs=3)
            if s < SLICES - 1:
                fetch_plain(s - 1, x)
                first_product(s + 1)
                angle_features_turned(s - 1, x)
            else:
                fetch(s - 1, x, 0, M)
                angle_features(s - 1, x, 0, M)
            if s + 3 < SLICES:
                load_chamber(s + 3)
            if s == 5:
                quantise_z(0, 0, M)
                deal(w3_w, w3_raw, 4)
            if s == 6:
                deal(w2_w, w2_raw, 8)
                deal(ws, ws_raw, 16)
            put(s)
        for c in range(len(CHUNKS)):
            far_early(c)

        last = SLICES - 1
        x = ring.tile([P, M], F32, name="x", bufs=3)
        n_chunks = len(CHUNKS)
        for step in range(n_chunks + 3):
            if step < n_chunks:
                lo, hi = starts[step], starts[step] + CHUNKS[step]
                fetch(last, x, lo, hi)
                angle_features(last, x, lo, hi, on_vector=step >= 2)
            c = step - 1
            if 0 <= c < n_chunks:
                quantise_z(1, starts[c], starts[c] + CHUNKS[c])
                far_last(c)
            c = step - 2
            if 0 <= c < n_chunks:
                far_out(c)
            c = step - 3
            if 0 <= c < n_chunks:
                far_planes(c)
        for q in range(4):
            nc.scalar.dma_start(out_2[0, 4 * q : 4 * q + 4, :].bitcast(I32), y_s[32 * q : 32 * q + 4, :].bitcast(I32))
